import numpy as np
import ml_dtypes


def mxq(x, axis, fmt="e4m3"):
    dtype, down = {"e4m3": (ml_dtypes.float8_e4m3fn, 7), "e5m2": (ml_dtypes.float8_e5m2, 14)}[fmt]
    v = np.moveaxis(np.asarray(x, np.float32).astype(ml_dtypes.bfloat16).astype(np.float64), axis, -1)
    blocks = v.reshape(v.shape[:-1] + (-1, 32))
    amax = np.abs(blocks).max(-1, keepdims=True)
    byte = np.maximum(np.where(amax > 0, np.frexp(amax)[1] - 1 + 127, 0) - down, 1)
    scale = np.exp2(byte - 127.0)
    codes = (blocks / scale).astype(np.float32).astype(dtype).astype(np.float64)
    return np.moveaxis((codes * scale).reshape(v.shape), -1, axis)


WIDE = False


def mx_kscale(k):
    if not WIDE:
        return np.ones(k)
    levels = np.array([10, -10, 5, -5, 0])
    if k % 512:
        return np.exp2(np.random.permutation(np.resize(levels, k // 32))).repeat(32)
    a = np.empty((k // 512, 16))
    for p in range(k // 512):
        a[p, :8] = np.random.permutation(np.resize(levels, 8))
        for g in range(8):
            far = levels[np.abs(levels - a[p, g]) >= 10]
            a[p, g + 8] = far[np.random.randint(len(far))]
    return np.exp2(a.ravel()).repeat(32)


def f64(x):
    return np.asarray(x).astype(np.float64)


def striped(idx):
    return np.tile(np.asarray(idx).reshape(-1, 16).T, (8, 1)).astype(np.uint16)


def unstriped(offs):
    return offs[:16].T.reshape(-1).astype(np.int64)


E2M1 = np.array([0.0, 0.5, 1.0, 1.5, 2.0, 3.0, 4.0, 6.0, -0.0, -0.5, -1.0, -1.5, -2.0, -3.0, -4.0, -6.0])


def pack_weight(w, fmt):
    k, n = w.shape
    w = f64(np.asarray(w, np.float32).astype(ml_dtypes.bfloat16)).reshape(k // 32, 32, n)
    amax = np.abs(w).max(1)
    if fmt == "e4m3":
        byte = np.frexp(amax)[1] - 1 + 127 - 7
    else:
        mant, ex = np.frexp(amax / 6.0)
        byte = np.where(mant > 0.5, ex, ex - 1) + 127
    byte = np.clip(np.where(amax > 0, byte, 1), 1, 254)
    scaled = (w * np.exp2(127.0 - byte)[:, None, :]).reshape(k, n).astype(np.float32)
    by_word = np.ascontiguousarray(scaled.reshape(k // 512, 128, 4, n).transpose(0, 1, 3, 2))
    if fmt == "e4m3":
        words = by_word.astype(ml_dtypes.float8_e4m3fn).view(np.uint8)
    else:
        c = by_word.astype(ml_dtypes.float4_e2m1fn).view(np.uint8) & 0xF
        words = (c[..., 0::2] | (c[..., 1::2] << 4)).reshape(k // 512, 128, 2 * n)
    return np.ascontiguousarray(words), np.ascontiguousarray(byte.astype(np.uint8).reshape(k // 512, 16, n))


def unpack_weight(words, scales, fmt):
    g, _, n = scales.shape
    words = np.ascontiguousarray(words).reshape(g, 128, n, -1)
    if fmt == "e4m3":
        vals = words.view(ml_dtypes.float8_e4m3fn).astype(np.float64)
    else:
        nib = np.empty((g, 128, n, 4), np.uint8)
        nib[..., 0::2] = words & 0xF
        nib[..., 1::2] = words >> 4
        vals = E2M1[nib]
    vals = vals * np.repeat(np.exp2(scales.astype(np.float64) - 127.0), 8, axis=1)[..., None]
    return vals.transpose(0, 1, 3, 2).reshape(g * 512, n)


def sigmoid(v):
    return 1.0 / (1.0 + np.exp(-v))


D, E, T, I, G, U, Q = 512, 512, 4096, 1024, 64, 512, 128


def setup_inputs():
    n = np.random.standard_normal
    idx = np.random.permutation(T)[:I]
    idx2 = np.random.permutation(U)[:G]
    fd = mx_kscale(D)
    fe = mx_kscale(E)
    keysp = pack_weight(n((D, T)) / fd[:, None], "e2m1")
    valsp = pack_weight(n((E, T)) / fe[:, None], "e2m1")
    return {
        "query": (n((D, Q)) * 0.7 / np.sqrt(D) * fd[:, None]).astype(np.float32),
        "keys_words": keysp[0],
        "keys_scales": keysp[1],
        "ptab": (n((Q, U)) * 1.0).astype(np.float32),
        "gout": (n((E, Q)) * 1 / np.sqrt(E) * fe[:, None]).astype(np.float32),
        "vals_words": valsp[0],
        "vals_scales": valsp[1],
        "lam": (np.random.uniform(0.5, 1.5, (Q, 1))).astype(np.float32),
        "old": (0.5 * n((Q, U))).astype(np.float32),
        "offs": striped(idx),
        "offs2": striped(idx2),
    }


def reference(query, keys_words, keys_scales, ptab, gout, vals_words, vals_scales, lam, old, offs, offs2):
    idx = unstriped(offs)
    idx2 = unstriped(offs2)
    keysu = unpack_weight(keys_words, keys_scales, "e2m1")
    valsu = unpack_weight(vals_words, vals_scales, "e2m1")
    queryq = mxq(f64(query), 0, "e4m3")
    keysidxg = keysu[:, idx]
    a = queryq.T @ keysidxg
    b = a.reshape(Q, G, I // G).mean(axis=2)
    tp = f64(ptab)[:, idx2] * f64(lam)
    gt = sigmoid(tp + b)
    gr = np.repeat(gt, I // G, axis=1)
    r = np.exp(a - np.max(a, axis=1, keepdims=True))
    p = r * gr
    z = np.sum(p, axis=1, keepdims=True)
    goutq = mxq(f64(gout), 0, "e4m3")
    valsidxg = valsu[:, idx]
    c0 = goutq.T @ valsidxg
    dz = np.sum(p * c0, axis=1, keepdims=True) / np.square(z) * (-1.0)
    dp = 1.0 / z * c0 + dz
    dgr = dp * r
    dgt = dgr.reshape(Q, G, I // G).sum(axis=2)
    dtp = dgt * gt * (1.0 - gt)
    gs = dtp * f64(lam) * 64.0
    gf = np.zeros((Q, U))
    gf[:, idx2] = gs
    y = f64(old) + gf
    return y

@@ -1,0 +1,211 @@
+from contextlib import ExitStack
+
+import concourse.mybir as mybir
+
+D, E, T, I, G, U, Q = 512, 512, 4096, 1024, 64, 512, 128
+FLOPS = 2 * Q * I * (D + E)
+
+F32 = mybir.dt.float32
+BF16 = mybir.dt.bfloat16
+I32 = mybir.dt.int32
+U32 = mybir.dt.uint32
+U16 = mybir.dt.uint16
+U8 = mybir.dt.uint8
+FP8X4 = mybir.dt.float8_e4m3fn_x4
+FP4X4 = mybir.dt.float4_e2m1fn_x4
+ALU = mybir.AluOpType
+ACT = mybir.ActivationFunctionType
+AXIS_X = mybir.AxisListType.X
+
+P = 128
+PACK = 4
+PAGE = I // G
+HALF = I // 2
+HALF_PAGES = G // 2
+LIST_COLS = HALF // 16
+
+
+def tile_attend_bpagelift_kernel(tc, query, keys_words, keys_scales, ptab, gout, vals_words, vals_scales, lam, old, offs, offs2, out):
+    nc = tc.nc
+    with ExitStack() as ctx:
+        sb = ctx.enter_context(tc.tile_pool(name="sb", bufs=1))
+        ps = ctx.enter_context(tc.psum_pool(name="ps", bufs=1))
+
+        def load_scale_rows(plane, scales):
+            for r in range(4):
+                nc.sync.dma_start(out=plane[:].bitcast(I32)[r:P:32, :], in_=scales[0].bitcast(I32)[r:16:4, :])
+
+        def quantise(raw, label, tag):
+            grouped = sb.tile([P, Q, PACK], BF16, name=label + "_grouped", tag=tag, align_bytes=64)
+            nc.scalar.copy(out=grouped[:], in_=raw[:].rearrange("p t q -> p q t"))
+            codes = sb.tile([P, Q], U32, name=label + "_codes", align_bytes=64)
+            plane = sb.tile([P, Q], U8, name=label + "_plane", align_bytes=64)
+            nc.vector.quantize_mx(out=codes[:].bitcast(FP8X4), scales=plane[:], in_=grouped[:].rearrange("p q t -> p (q t)"))
+            return codes, plane
+
+        def half_list(h):
+            return slots[:, h * LIST_COLS : (h + 1) * LIST_COLS]
+
+        def mx_product(bank, stationary, words, plane, h):
+            codes, code_plane = stationary
+            nc.tensor.matmul_mx(
+                out=bank[:],
+                lhsT=codes[:].bitcast(FP8X4),
+                lhsT_scale=code_plane[:],
+                rhs=words.bitcast(FP4X4),
+                rhs_scale=plane[:, h * HALF : (h + 1) * HALF],
+                start=True,
+                stop=True,
+            )
+
+        key_plane = sb.tile([P, T], U8, name="key_plane", tag="key_plane_then_val_pool")
+        nc.vector.memset(key_plane[:].bitcast(I32), 0)
+        slots = sb.tile([P, I // 16], U16, name="slots")
+        nc.sync.dma_start(slots[:], offs)
+        pages = sb.tile([P, G // 16], U16, name="pages")
+        nc.sync.dma_start(pages[:], offs2)
+        query_raw = sb.tile([P, PACK, Q], F32, name="query_raw", tag="query_then_gout")
+        nc.scalar.dma_start(out=query_raw[:], in_=query.rearrange("(p t) q -> p t q", t=PACK))
+        lam_sb = sb.tile([P, 1], F32, name="lam_sb")
+        nc.gpsimd.dma_start(out=lam_sb[:], in_=lam)
+        load_scale_rows(key_plane, keys_scales)
+
+        zeros = sb.tile([P, P], F32, name="zeros", tag="zeros_key_pool_old")
+        nc.vector.memset(zeros[:], 0.0)
+        ident = sb.tile([P, P], F32, name="ident")
+        nc.gpsimd.affine_select(out=ident[:], in_=zeros[:], compare_op=ALU.not_equal, fill=1.0, base=0, pattern=[[-1, P]], channel_multiplier=1)
+        key_pool = sb.tile([P, T], U16, name="key_pool", tag="zeros_key_pool_old")
+        nc.sync.dma_start(out=key_pool[:].bitcast(I32), in_=keys_words[0].bitcast(I32))
+
+        val_plane = sb.tile([P, T], U8, name="val_plane")
+        nc.vector.memset(val_plane[:].bitcast(I32), 0)
+        load_scale_rows(val_plane, vals_scales)
+        placed = sb.tile([P, U], F32, name="placed")
+        nc.vector.memset(placed[:], 0.0)
+        lift = sb.tile([P, 2 * G], F32, name="lift")
+        nc.vector.memset(lift[:, G:], 0.0)
+
+        key_bytes = sb.tile([P, I], U8, name="key_bytes", align_bytes=64)
+        nc.vector.tensor_copy(key_bytes[:], key_plane[:].indirect(slots[:]))
+        query_mx = quantise(query_raw, "query", "grouped_then_ptab")
+        ptab_sb = sb.tile([P, U], F32, name="ptab_sb", tag="grouped_then_ptab", align_bytes=64)
+        nc.sync.dma_start(out=ptab_sb[:], in_=ptab)
+        gout_raw = sb.tile([P, PACK, Q], F32, name="gout_raw", tag="query_then_gout")
+        nc.sync.dma_start(out=gout_raw[:], in_=gout.rearrange("(p t) q -> p t q", t=PACK))
+        val_pool = sb.tile([P, T], U16, name="val_pool", tag="key_plane_then_val_pool")
+        nc.sync.dma_start(out=val_pool[:].bitcast(I32), in_=vals_words[0].bitcast(I32))
+        score = []
+        for h in range(2):
+            key_words = sb.tile([P, HALF], U16, name="key_words%d" % h, align_bytes=64)
+            nc.vector.tensor_copy(key_words[:], key_pool[:].indirect(half_list(h)))
+            bank = ps.tile([P, HALF], F32, name="score%d" % h)
+            mx_product(bank, query_mx, key_words[:], key_bytes, h)
+            score.append(bank)
+
+        old_sb = sb.tile([P, U], F32, name="old_sb", tag="zeros_key_pool_old")
+        nc.sync.dma_start(out=old_sb[:], in_=old)
+
+        pairs = sb.tile([P, PAGE, 2 * G], F32, name="pairs")
+        neg_max_first = sb.tile([P, 1], F32, name="neg_max_first", tag="before_val_bytes", align_bytes=64)
+        neg_max = sb.tile([P, 1], F32, name="neg_max", tag="before_val_words", align_bytes=64)
+
+        def negate_scores(h, start, result):
+            nc.vector.tensor_scalar(
+                out=pairs[:, :, h * HALF_PAGES : (h + 1) * HALF_PAGES],
+                in0=score[h][:].rearrange("p (g j) -> p j g", j=PAGE),
+                scalar1=-1.0,
+                scalar2=start,
+                op0=ALU.mult,
+                op1=ALU.min,
+                accum_out=result[:],
+            )
+
+        negate_scores(0, None, neg_max_first)
+        picked = sb.tile([P, G], F32, name="picked")
+        nc.vector.tensor_copy(picked[:], ptab_sb[:].indirect(pages[:]))
+        negate_scores(1, neg_max_first[:], neg_max)
+        gout_mx = quantise(gout_raw, "gout", "gout_grouped")
+
+        lam_page = sb.tile([P, 1], F32, name="lam_page")
+        nc.scalar.mul(lam_page[:], lam_sb[:], -float(PAGE))
+        lam_out = sb.tile([P, 1], F32, name="lam_out")
+        nc.scalar.mul(lam_out[:], lam_sb[:], 64.0)
+        neg_lam_out = sb.tile([P, 1], F32, name="neg_lam_out")
+        nc.scalar.mul(neg_lam_out[:], lam_sb[:], -64.0)
+
+        nc.scalar.activation(out=pairs[:, :, G:], in_=pairs[:, :, :G], func=ACT.Exp, bias=neg_max[:], scale=-1.0)
+        nc.scalar.activation(out=lift[:, :G], in_=picked[:], func=ACT.Copy, scale=lam_page[:])
+        weight = []
+        for h in range(2):
+            r_half = sb.tile([P, HALF], F32, name="weight%d" % h)
+            nc.scalar.activation(out=r_half[:], in_=score[h][:], func=ACT.Exp, bias=neg_max[:], scale=1.0)
+            weight.append(r_half)
+
+        turned = ps.tile([P, P], F32, name="turned", tag="turned_then_second")
+        for j in range(PAGE):
+            nc.tensor.matmul(turned[:], lhsT=pairs[:, j, :], rhs=ident[:], is_transpose=True, start=(j == 0), stop=False)
+        nc.tensor.matmul(turned[:], lhsT=lift[:], rhs=ident[:], is_transpose=True, start=False, stop=True)
+
+        val_bytes = sb.tile([P, I], U8, name="val_bytes", tag="before_val_bytes", align_bytes=64)
+        nc.vector.tensor_copy(val_bytes[:], val_plane[:].indirect(slots[:]))
+        val_words = sb.tile([P, I], U16, name="val_words", tag="before_val_words", align_bytes=64)
+        nc.vector.tensor_copy(val_words[:, :HALF], val_pool[:].indirect(half_list(0)))
+        back0 = ps.tile([P, HALF], F32, name="back0")
+        mx_product(back0, gout_mx, val_words[:, :HALF], val_bytes, 0)
+
+        turned_sb = sb.tile([P, P], F32, name="turned_sb")
+        nc.scalar.activation(out=turned_sb[:G, :], in_=turned[:G, :], func=ACT.Sigmoid, scale=-1.0 / PAGE)
+        nc.scalar.copy(out=turned_sb[G:, :], in_=turned[G:, :])
+        by_row = ps.tile([P, P], F32, name="by_row")
+        nc.tensor.transpose(by_row[:], turned_sb[:], ident[:])
+
+        nc.vector.tensor_copy(val_words[:, HALF:], val_pool[:].indirect(half_list(1)))
+        back1 = ps.tile([P, HALF], F32, name="back1", tag="turned_then_second")
+        mx_product(back1, gout_mx, val_words[:, HALF:], val_bytes, 1)
+        back = [back0, back1]
+
+        gate = sb.tile([P, G], F32, name="gate")
+        nc.scalar.copy(out=gate[:], in_=by_row[:, :G])
+        slope = sb.tile([P, G], F32, name="slope")
+        nc.scalar.activation(out=slope[:], in_=gate[:], func=ACT.Identity, bias=lam_out[:], scale=neg_lam_out[:])
+
+        page_dot = sb.tile([P, G], F32, name="page_dot")
+        prod = [sb.tile([P, HALF], F32, name="prod%d" % h) for h in range(2)]
+
+        def multiply(h):
+            nc.vector.tensor_tensor(out=prod[h][:], in0=back[h][:], in1=weight[h][:], op=ALU.mult)
+
+        def sum_pages(h):
+            nc.vector.tensor_reduce(
+                out=page_dot[:, h * HALF_PAGES : (h + 1) * HALF_PAGES],
+                in_=prod[h][:].rearrange("p (g j) -> p g j", j=PAGE),
+                axis=AXIS_X,
+                op=ALU.add,
+            )
+
+        multiply(0)
+        mass = sb.tile([P, G], F32, name="mass")
+        total = sb.tile([P, 1], F32, name="total")
+        nc.vector.scalar_tensor_tensor(out=mass[:], in0=by_row[:, G:], scalar=1.0, in1=gate[:], op0=ALU.mult, op1=ALU.mult, accum_out=total[:])
+        sum_pages(0)
+        inv_total = sb.tile([P, 1], F32, name="inv_total")
+        nc.vector.reciprocal(inv_total[:], total[:])
+        share = sb.tile([P, G], F32, name="share")
+        nc.scalar.activation(out=share[:], in_=mass[:], func=ACT.Copy, scale=inv_total[:])
+        factor = sb.tile([P, G], F32, name="factor")
+        nc.scalar.activation(out=factor[:], in_=slope[:], func=ACT.Copy, scale=inv_total[:])
+        multiply(1)
+        sum_pages(1)
+
+        neg_gated = sb.tile([P, G], F32, name="neg_gated")
+        neg_dot = sb.tile([P, 1], F32, name="neg_dot")
+        nc.vector.scalar_tensor_tensor(out=neg_gated[:], in0=page_dot[:], scalar=-1.0, in1=gate[:], op0=ALU.mult, op1=ALU.mult, accum_out=neg_dot[:])
+        centred = sb.tile([P, G], F32, name="centred")
+        nc.vector.scalar_tensor_tensor(out=centred[:], in0=share[:], scalar=neg_dot[:], in1=neg_gated[:], op0=ALU.mult, op1=ALU.subtract)
+        nc.vector.tensor_tensor(placed[:].indirect(pages[:]), centred[:], factor[:], ALU.mult)
+
+        for h, queue in enumerate((nc.sync, nc.scalar)):
+            cols = slice(h * U // 2, (h + 1) * U // 2)
+            result = sb.tile([P, U // 2], F32, name="result%d" % h)
+            nc.vector.tensor_tensor(out=result[:], in0=placed[:, cols], in1=old_sb[:, cols], op=ALU.add)
+            queue.dma_start(out=out[:, cols], in_=result[:])

@@ -1,6 +1,7 @@
 from contextlib import ExitStack
 
 import concourse.mybir as mybir
+from concourse.masks import make_identity
 
 D, E, T, I, G, U, Q = 512, 512, 4096, 1024, 64, 512, 128
 FLOPS = 2 * Q * I * (D + E)
@@ -35,79 +36,76 @@ def tile_attend_bpagelift_kernel(tc, query, keys_words, keys_scales, ptab, gout,
             for r in range(4):
                 nc.sync.dma_start(out=plane[:].bitcast(I32)[r:P:32, :], in_=scales[0].bitcast(I32)[r:16:4, :])
 
-        def quantise(raw, label, tag):
-            grouped = sb.tile([P, Q, PACK], BF16, name=label + "_grouped", tag=tag, align_bytes=64)
+        def quantise(raw, label, plane_tag):
+            grouped = sb.tile([P, Q, PACK], BF16, name=label + "_grouped", align_bytes=64)
             nc.scalar.copy(out=grouped[:], in_=raw[:].rearrange("p t q -> p q t"))
             codes = sb.tile([P, Q], U32, name=label + "_codes", align_bytes=64)
-            plane = sb.tile([P, Q], U8, name=label + "_plane", align_bytes=64)
+            plane = sb.tile([P, Q], U8, name=label + "_plane", tag=plane_tag, align_bytes=64)
             nc.vector.quantize_mx(out=codes[:].bitcast(FP8X4), scales=plane[:], in_=grouped[:].rearrange("p q t -> p (q t)"))
             return codes, plane
 
         def half_list(h):
             return slots[:, h * LIST_COLS : (h + 1) * LIST_COLS]
 
-        def mx_product(bank, stationary, words, plane, h):
+        def mx_product(bank, stationary, words, plane):
             codes, code_plane = stationary
             nc.tensor.matmul_mx(
                 out=bank[:],
                 lhsT=codes[:].bitcast(FP8X4),
                 lhsT_scale=code_plane[:],
                 rhs=words.bitcast(FP4X4),
-                rhs_scale=plane[:, h * HALF : (h + 1) * HALF],
+                rhs_scale=plane,
                 start=True,
                 stop=True,
             )
 
-        key_plane = sb.tile([P, T], U8, name="key_plane", tag="key_plane_then_val_pool")
+        key_plane = sb.tile([P, T], U8, name="key_plane")
         nc.vector.memset(key_plane[:].bitcast(I32), 0)
-        slots = sb.tile([P, I // 16], U16, name="slots")
-        nc.sync.dma_start(slots[:], offs)
-        pages = sb.tile([P, G // 16], U16, name="pages")
-        nc.sync.dma_start(pages[:], offs2)
-        query_raw = sb.tile([P, PACK, Q], F32, name="query_raw", tag="query_then_gout")
-        nc.scalar.dma_start(out=query_raw[:], in_=query.rearrange("(p t) q -> p t q", t=PACK))
-        lam_sb = sb.tile([P, 1], F32, name="lam_sb")
-        nc.gpsimd.dma_start(out=lam_sb[:], in_=lam)
-        load_scale_rows(key_plane, keys_scales)
-
-        zeros = sb.tile([P, P], F32, name="zeros", tag="zeros_key_pool_old")
-        nc.vector.memset(zeros[:], 0.0)
-        ident = sb.tile([P, P], F32, name="ident")
-        nc.gpsimd.affine_select(out=ident[:], in_=zeros[:], compare_op=ALU.not_equal, fill=1.0, base=0, pattern=[[-1, P]], channel_multiplier=1)
-        key_pool = sb.tile([P, T], U16, name="key_pool", tag="zeros_key_pool_old")
-        nc.sync.dma_start(out=key_pool[:].bitcast(I32), in_=keys_words[0].bitcast(I32))
-
         val_plane = sb.tile([P, T], U8, name="val_plane")
         nc.vector.memset(val_plane[:].bitcast(I32), 0)
+        key_pool = sb.tile([P, T], U16, name="key_pool")
+        nc.sync.dma_start(out=key_pool[:].bitcast(I32), in_=keys_words[0].bitcast(I32))
+        slots = sb.tile([P, I // 16], U16, name="slots")
+        nc.sync.dma_start(slots[:], offs)
+        query_raw = sb.tile([P, PACK, Q], F32, name="query_raw")
+        nc.sync.dma_start(out=query_raw[:], in_=query.rearrange("(p t) q -> p t q", t=PACK))
+        gout_raw = sb.tile([P, PACK, Q], F32, name="gout_raw")
+        nc.sync.dma_start(out=gout_raw[:], in_=gout.rearrange("(p t) q -> p t q", t=PACK))
+        load_scale_rows(key_plane, keys_scales)
+        ptab_sb = sb.tile([P, U], F32, name="ptab_sb")
+        nc.sync.dma_start(out=ptab_sb[:], in_=ptab)
+        pages = sb.tile([P, G // 16], U16, name="pages")
+        nc.sync.dma_start(pages[:], offs2)
+        lam_sb = sb.tile([P, 1], F32, name="lam_sb")
+        nc.sync.dma_start(out=lam_sb[:], in_=lam)
         load_scale_rows(val_plane, vals_scales)
+        val_pool = sb.tile([P, T], U16, name="val_pool")
+        nc.sync.dma_start(out=val_pool[:].bitcast(I32), in_=vals_words[0].bitcast(I32))
+        old_sb = sb.tile([P, U], F32, name="old_sb")
+        nc.sync.dma_start(out=old_sb[:], in_=old)
+
         placed = sb.tile([P, U], F32, name="placed")
         nc.vector.memset(placed[:], 0.0)
         lift = sb.tile([P, 2 * G], F32, name="lift")
         nc.vector.memset(lift[:, G:], 0.0)
+        ident = sb.tile([P, P], F32, name="ident")
+        make_identity(nc, ident[:])
 
-        key_bytes = sb.tile([P, I], U8, name="key_bytes", align_bytes=64)
-        nc.vector.tensor_copy(key_bytes[:], key_plane[:].indirect(slots[:]))
-        query_mx = quantise(query_raw, "query", "grouped_then_ptab")
-        ptab_sb = sb.tile([P, U], F32, name="ptab_sb", tag="grouped_then_ptab", align_bytes=64)
-        nc.sync.dma_start(out=ptab_sb[:], in_=ptab)
-        gout_raw = sb.tile([P, PACK, Q], F32, name="gout_raw", tag="query_then_gout")
-        nc.sync.dma_start(out=gout_raw[:], in_=gout.rearrange("(p t) q -> p t q", t=PACK))
-        val_pool = sb.tile([P, T], U16, name="val_pool", tag="key_plane_then_val_pool")
-        nc.sync.dma_start(out=val_pool[:].bitcast(I32), in_=vals_words[0].bitcast(I32))
+        key_words = sb.tile([P, I], U16, name="key_words", align_bytes=64)
+        nc.vector.tensor_copy(key_words[:], key_pool[:].indirect(slots[:]))
+        query_mx = quantise(query_raw, "query", "query_plane")
         score = []
         for h in range(2):
-            key_words = sb.tile([P, HALF], U16, name="key_words%d" % h, align_bytes=64)
-            nc.vector.tensor_copy(key_words[:], key_pool[:].indirect(half_list(h)))
+            key_bytes = sb.tile([P, HALF], U8, name="key_bytes%d" % h, tag="key_bytes%d" % h, align_bytes=64)
+            nc.vector.tensor_copy(key_bytes[:], key_plane[:].indirect(half_list(h)))
             bank = ps.tile([P, HALF], F32, name="score%d" % h)
-            mx_product(bank, query_mx, key_words[:], key_bytes, h)
+            mx_product(bank, query_mx, key_words[:, h * HALF : (h + 1) * HALF], key_bytes[:])
             score.append(bank)
 
-        old_sb = sb.tile([P, U], F32, name="old_sb", tag="zeros_key_pool_old")
-        nc.sync.dma_start(out=old_sb[:], in_=old)
-
         pairs = sb.tile([P, PAGE, 2 * G], F32, name="pairs")
-        neg_max_first = sb.tile([P, 1], F32, name="neg_max_first", tag="before_val_bytes", align_bytes=64)
-        neg_max = sb.tile([P, 1], F32, name="neg_max", tag="before_val_words", align_bytes=64)
+        neg_max_first = sb.tile([P, 1], F32, name="neg_max_first")
+        neg_max_tile = sb.tile([P, 1], F32, name="neg_max")
+        neg_max = neg_max_tile[:]
 
         def negate_scores(h, start, result):
             nc.vector.tensor_scalar(
@@ -117,14 +115,14 @@ def tile_attend_bpagelift_kernel(tc, query, keys_words, keys_scales, ptab, gout,
                 scalar2=start,
                 op0=ALU.mult,
                 op1=ALU.min,
-                accum_out=result[:],
+                accum_out=result,
             )
 
-        negate_scores(0, None, neg_max_first)
+        negate_scores(0, None, neg_max_first[:])
         picked = sb.tile([P, G], F32, name="picked")
         nc.vector.tensor_copy(picked[:], ptab_sb[:].indirect(pages[:]))
         negate_scores(1, neg_max_first[:], neg_max)
-        gout_mx = quantise(gout_raw, "gout", "gout_grouped")
+        gout_mx = quantise(gout_raw, "gout", "key_bytes0")
 
         lam_page = sb.tile([P, 1], F32, name="lam_page")
         nc.scalar.mul(lam_page[:], lam_sb[:], -float(PAGE))
@@ -133,36 +131,36 @@ def tile_attend_bpagelift_kernel(tc, query, keys_words, keys_scales, ptab, gout,
         neg_lam_out = sb.tile([P, 1], F32, name="neg_lam_out")
         nc.scalar.mul(neg_lam_out[:], lam_sb[:], -64.0)
 
-        nc.scalar.activation(out=pairs[:, :, G:], in_=pairs[:, :, :G], func=ACT.Exp, bias=neg_max[:], scale=-1.0)
+        nc.scalar.activation(out=pairs[:, :, G:], in_=pairs[:, :, :G], func=ACT.Exp, bias=neg_max, scale=-1.0)
         nc.scalar.activation(out=lift[:, :G], in_=picked[:], func=ACT.Copy, scale=lam_page[:])
         weight = []
         for h in range(2):
-            r_half = sb.tile([P, HALF], F32, name="weight%d" % h)
-            nc.scalar.activation(out=r_half[:], in_=score[h][:], func=ACT.Exp, bias=neg_max[:], scale=1.0)
+            r_half = sb.tile([P, HALF], F32, name="weight%d" % h, tag="weight%d" % h)
+            nc.scalar.activation(out=r_half[:], in_=score[h][:], func=ACT.Exp, bias=neg_max, scale=1.0)
             weight.append(r_half)
 
-        turned = ps.tile([P, P], F32, name="turned", tag="turned_then_second")
+        turned = ps.tile([P, P], F32, name="turned")
         for j in range(PAGE):
             nc.tensor.matmul(turned[:], lhsT=pairs[:, j, :], rhs=ident[:], is_transpose=True, start=(j == 0), stop=False)
         nc.tensor.matmul(turned[:], lhsT=lift[:], rhs=ident[:], is_transpose=True, start=False, stop=True)
 
-        val_bytes = sb.tile([P, I], U8, name="val_bytes", tag="before_val_bytes", align_bytes=64)
+        val_bytes = sb.tile([P, I], U8, name="val_bytes", align_bytes=64)
         nc.vector.tensor_copy(val_bytes[:], val_plane[:].indirect(slots[:]))
-        val_words = sb.tile([P, I], U16, name="val_words", tag="before_val_words", align_bytes=64)
-        nc.vector.tensor_copy(val_words[:, :HALF], val_pool[:].indirect(half_list(0)))
+        val_words = [sb.tile([P, HALF], U16, name="val_words%d" % h, tag="val_words%d" % h, align_bytes=64) for h in range(2)]
+        nc.vector.tensor_copy(val_words[0][:], val_pool[:].indirect(half_list(0)))
         back0 = ps.tile([P, HALF], F32, name="back0")
-        mx_product(back0, gout_mx, val_words[:, :HALF], val_bytes, 0)
+        mx_product(back0, gout_mx, val_words[0][:], val_bytes[:, :HALF])
 
-        turned_sb = sb.tile([P, P], F32, name="turned_sb")
+        nc.vector.tensor_copy(val_words[1][:], val_pool[:].indirect(half_list(1)))
+        back1 = ps.tile([P, HALF], F32, name="back1")
+        mx_product(back1, gout_mx, val_words[1][:], val_bytes[:, HALF:])
+        back = [back0, back1]
+
+        turned_sb = sb.tile([P, P], F32, name="turned_sb", tag="val_words0", align_bytes=64)
         nc.scalar.activation(out=turned_sb[:G, :], in_=turned[:G, :], func=ACT.Sigmoid, scale=-1.0 / PAGE)
         nc.scalar.copy(out=turned_sb[G:, :], in_=turned[G:, :])
         by_row = ps.tile([P, P], F32, name="by_row")
         nc.tensor.transpose(by_row[:], turned_sb[:], ident[:])
-
-        nc.vector.tensor_copy(val_words[:, HALF:], val_pool[:].indirect(half_list(1)))
-        back1 = ps.tile([P, HALF], F32, name="back1", tag="turned_then_second")
-        mx_product(back1, gout_mx, val_words[:, HALF:], val_bytes, 1)
-        back = [back0, back1]
 
         gate = sb.tile([P, G], F32, name="gate")
         nc.scalar.copy(out=gate[:], in_=by_row[:, :G])
@@ -184,18 +182,18 @@ def tile_attend_bpagelift_kernel(tc, query, keys_words, keys_scales, ptab, gout,
             )
 
         multiply(0)
-        mass = sb.tile([P, G], F32, name="mass")
+        sum_pages(0)
+        multiply(1)
+        mass = sb.tile([P, G], F32, name="mass", tag="weight1")
         total = sb.tile([P, 1], F32, name="total")
         nc.vector.scalar_tensor_tensor(out=mass[:], in0=by_row[:, G:], scalar=1.0, in1=gate[:], op0=ALU.mult, op1=ALU.mult, accum_out=total[:])
-        sum_pages(0)
+        sum_pages(1)
         inv_total = sb.tile([P, 1], F32, name="inv_total")
         nc.vector.reciprocal(inv_total[:], total[:])
         share = sb.tile([P, G], F32, name="share")
         nc.scalar.activation(out=share[:], in_=mass[:], func=ACT.Copy, scale=inv_total[:])
         factor = sb.tile([P, G], F32, name="factor")
         nc.scalar.activation(out=factor[:], in_=slope[:], func=ACT.Copy, scale=inv_total[:])
-        multiply(1)
-        sum_pages(1)
 
         neg_gated = sb.tile([P, G], F32, name="neg_gated")
         neg_dot = sb.tile([P, 1], F32, name="neg_dot")

@@ -59,25 +59,38 @@ def tile_attend_bpagelift_kernel(tc, query, keys_words, keys_scales, ptab, gout,
                 stop=True,
             )
 
-        key_plane = sb.tile([P, T], U8, name="key_plane")
-        nc.vector.memset(key_plane[:].bitcast(I32), 0)
-        val_plane = sb.tile([P, T], U8, name="val_plane")
-        nc.vector.memset(val_plane[:].bitcast(I32), 0)
-        key_pool = sb.tile([P, T], U16, name="key_pool")
-        nc.sync.dma_start(out=key_pool[:].bitcast(I32), in_=keys_words[0].bitcast(I32))
+        key_rows = sb.tile([P, T], U8, name="key_rows", tag="key_rows_then_query_plane", align_bytes=64)
+        nc.vector.memset(key_rows[:].bitcast(I32), 0)
         slots = sb.tile([P, I // 16], U16, name="slots")
         nc.sync.dma_start(slots[:], offs)
         query_raw = sb.tile([P, PACK, Q], F32, name="query_raw")
-        nc.sync.dma_start(out=query_raw[:], in_=query.rearrange("(p t) q -> p t q", t=PACK))
-        gout_raw = sb.tile([P, PACK, Q], F32, name="gout_raw")
-        nc.sync.dma_start(out=gout_raw[:], in_=gout.rearrange("(p t) q -> p t q", t=PACK))
-        load_scale_rows(key_plane, keys_scales)
-        ptab_sb = sb.tile([P, U], F32, name="ptab_sb")
-        nc.sync.dma_start(out=ptab_sb[:], in_=ptab)
+        nc.scalar.dma_start(out=query_raw[:], in_=query.rearrange("(p t) q -> p t q", t=PACK))
         pages = sb.tile([P, G // 16], U16, name="pages")
         nc.sync.dma_start(pages[:], offs2)
         lam_sb = sb.tile([P, 1], F32, name="lam_sb")
         nc.sync.dma_start(out=lam_sb[:], in_=lam)
+        nc.sync.dma_start(out=key_rows[:].bitcast(I32)[0:P:8, :], in_=keys_scales[0].bitcast(I32))
+        key_pool = sb.tile([P, T], U16, name="key_pool")
+        nc.sync.dma_start(out=key_pool[:].bitcast(I32), in_=keys_words[0].bitcast(I32))
+        gout_raw = sb.tile([P, PACK, Q], F32, name="gout_raw")
+        nc.sync.dma_start(out=gout_raw[:], in_=gout.rearrange("(p t) q -> p t q", t=PACK))
+
+        def pick_key_scales(h):
+            key_bytes = sb.tile([P, HALF], U8, name="key_bytes%d" % h)
+            nc.vector.tensor_copy(key_bytes[:], key_rows[:].indirect(half_list(h)))
+            plane = sb.tile([P, HALF], U8, name="key_plane%d" % h, align_bytes=64)
+            nc.vector.memset(plane[:].bitcast(I32), 0)
+            for r in range(4):
+                nc.sync.dma_start(out=plane[:].bitcast(I32)[r:P:32, :], in_=key_bytes[:].bitcast(I32)[8 * r : P : 32, :])
+            return plane
+
+        key_planes = [pick_key_scales(0)]
+        ptab_sb = sb.tile([P, U], F32, name="ptab_sb")
+        nc.sync.dma_start(out=ptab_sb[:], in_=ptab)
+        key_planes.append(pick_key_scales(1))
+
+        val_plane = sb.tile([P, T], U8, name="val_plane")
+        nc.vector.memset(val_plane[:].bitcast(I32), 0)
         load_scale_rows(val_plane, vals_scales)
         val_pool = sb.tile([P, T], U16, name="val_pool")
         nc.sync.dma_start(out=val_pool[:].bitcast(I32), in_=vals_words[0].bitcast(I32))
@@ -91,15 +104,13 @@ def tile_attend_bpagelift_kernel(tc, query, keys_words, keys_scales, ptab, gout,
         ident = sb.tile([P, P], F32, name="ident")
         make_identity(nc, ident[:])
 
-        key_words = sb.tile([P, I], U16, name="key_words", align_bytes=64)
-        nc.vector.tensor_copy(key_words[:], key_pool[:].indirect(slots[:]))
-        query_mx = quantise(query_raw, "query", "query_plane")
+        query_mx = quantise(query_raw, "query", "key_rows_then_query_plane")
         score = []
         for h in range(2):
-            key_bytes = sb.tile([P, HALF], U8, name="key_bytes%d" % h, tag="key_bytes%d" % h, align_bytes=64)
-            nc.vector.tensor_copy(key_bytes[:], key_plane[:].indirect(half_list(h)))
+            key_words = sb.tile([P, HALF], U16, name="key_words%d" % h, align_bytes=64)
+            nc.vector.tensor_copy(key_words[:], key_pool[:].indirect(half_list(h)))
             bank = ps.tile([P, HALF], F32, name="score%d" % h)
-            mx_product(bank, query_mx, key_words[:, h * HALF : (h + 1) * HALF], key_bytes[:])
+            mx_product(bank, query_mx, key_words[:], key_planes[h][:])
             score.append(bank)
 
         pairs = sb.tile([P, PAGE, 2 * G], F32, name="pairs")
@@ -122,7 +133,7 @@ def tile_attend_bpagelift_kernel(tc, query, keys_words, keys_scales, ptab, gout,
         picked = sb.tile([P, G], F32, name="picked")
         nc.vector.tensor_copy(picked[:], ptab_sb[:].indirect(pages[:]))
         negate_scores(1, neg_max_first[:], neg_max)
-        gout_mx = quantise(gout_raw, "gout", "key_bytes0")
+        gout_mx = quantise(gout_raw, "gout", "gout_plane")
 
         lam_page = sb.tile([P, 1], F32, name="lam_page")
         nc.scalar.mul(lam_page[:], lam_sb[:], -float(PAGE))
@@ -131,7 +142,8 @@ def tile_attend_bpagelift_kernel(tc, query, keys_words, keys_scales, ptab, gout,
         neg_lam_out = sb.tile([P, 1], F32, name="neg_lam_out")
         nc.scalar.mul(neg_lam_out[:], lam_sb[:], -64.0)
 
-        nc.scalar.activation(out=pairs[:, :, G:], in_=pairs[:, :, :G], func=ACT.Exp, bias=neg_max, scale=-1.0)
+        for first in range(0, PAGE, 4):
+            nc.scalar.activation(out=pairs[:, first : first + 4, G:], in_=pairs[:, first : first + 4, :G], func=ACT.Exp, bias=neg_max, scale=-1.0)
         nc.scalar.activation(out=lift[:, :G], in_=picked[:], func=ACT.Copy, scale=lam_page[:])
         weight = []
         for h in range(2):

@@ -64,11 +64,9 @@ def tile_attend_bpagelift_kernel(tc, query, keys_words, keys_scales, ptab, gout,
         slots = sb.tile([P, I // 16], U16, name="slots")
         nc.sync.dma_start(slots[:], offs)
         query_raw = sb.tile([P, PACK, Q], F32, name="query_raw")
-        nc.scalar.dma_start(out=query_raw[:], in_=query.rearrange("(p t) q -> p t q", t=PACK))
+        nc.sync.dma_start(out=query_raw[:], in_=query.rearrange("(p t) q -> p t q", t=PACK))
         pages = sb.tile([P, G // 16], U16, name="pages")
         nc.sync.dma_start(pages[:], offs2)
-        lam_sb = sb.tile([P, 1], F32, name="lam_sb")
-        nc.sync.dma_start(out=lam_sb[:], in_=lam)
         nc.sync.dma_start(out=key_rows[:].bitcast(I32)[0:P:8, :], in_=keys_scales[0].bitcast(I32))
         key_pool = sb.tile([P, T], U16, name="key_pool")
         nc.sync.dma_start(out=key_pool[:].bitcast(I32), in_=keys_words[0].bitcast(I32))
@@ -92,6 +90,8 @@ def tile_attend_bpagelift_kernel(tc, query, keys_words, keys_scales, ptab, gout,
         val_plane = sb.tile([P, T], U8, name="val_plane")
         nc.vector.memset(val_plane[:].bitcast(I32), 0)
         load_scale_rows(val_plane, vals_scales)
+        lam_sb = sb.tile([P, 1], F32, name="lam_sb")
+        nc.sync.dma_start(out=lam_sb[:], in_=lam)
         val_pool = sb.tile([P, T], U16, name="val_pool")
         nc.sync.dma_start(out=val_pool[:].bitcast(I32), in_=vals_words[0].bitcast(I32))
         old_sb = sb.tile([P, U], F32, name="old_sb")

from contextlib import ExitStack

import concourse.mybir as mybir
from concourse.masks import make_identity

D, E, T, I, G, U, Q = 512, 512, 4096, 1024, 64, 512, 128
FLOPS = 2 * Q * I * (D + E)

F32 = mybir.dt.float32
BF16 = mybir.dt.bfloat16
I32 = mybir.dt.int32
U32 = mybir.dt.uint32
U16 = mybir.dt.uint16
U8 = mybir.dt.uint8
FP8X4 = mybir.dt.float8_e4m3fn_x4
FP4X4 = mybir.dt.float4_e2m1fn_x4
ALU = mybir.AluOpType
ACT = mybir.ActivationFunctionType
AXIS_X = mybir.AxisListType.X

P = 128
PACK = 4
PAGE = I // G
HALF = I // 2
HALF_PAGES = G // 2
LIST_COLS = HALF // 16


def tile_attend_bpagelift_kernel(tc, query, keys_words, keys_scales, ptab, gout, vals_words, vals_scales, lam, old, offs, offs2, out):
    nc = tc.nc
    with ExitStack() as ctx:
        sb = ctx.enter_context(tc.tile_pool(name="sb", bufs=1))
        ps = ctx.enter_context(tc.psum_pool(name="ps", bufs=1))

        def load_scale_rows(plane, scales):
            for r in range(4):
                nc.sync.dma_start(out=plane[:].bitcast(I32)[r:P:32, :], in_=scales[0].bitcast(I32)[r:16:4, :])

        def quantise(raw, label, plane_tag):
            grouped = sb.tile([P, Q, PACK], BF16, name=label + "_grouped", align_bytes=64)
            nc.scalar.copy(out=grouped[:], in_=raw[:].rearrange("p t q -> p q t"))
            codes = sb.tile([P, Q], U32, name=label + "_codes", align_bytes=64)
            plane = sb.tile([P, Q], U8, name=label + "_plane", tag=plane_tag, align_bytes=64)
            nc.vector.quantize_mx(out=codes[:].bitcast(FP8X4), scales=plane[:], in_=grouped[:].rearrange("p q t -> p (q t)"))
            return codes, plane

        def half_list(h):
            return slots[:, h * LIST_COLS : (h + 1) * LIST_COLS]

        def mx_product(bank, stationary, words, plane):
            codes, code_plane = stationary
            nc.tensor.matmul_mx(
                out=bank[:],
                lhsT=codes[:].bitcast(FP8X4),
                lhsT_scale=code_plane[:],
                rhs=words.bitcast(FP4X4),
                rhs_scale=plane,
                start=True,
                stop=True,
            )

        key_rows = sb.tile([P, T], U8, name="key_rows", tag="key_rows_then_query_plane", align_bytes=64)
        nc.vector.memset(key_rows[:].bitcast(I32), 0)
        slots = sb.tile([P, I // 16], U16, name="slots")
        nc.sync.dma_start(slots[:], offs)
        query_raw = sb.tile([P, PACK, Q], F32, name="query_raw")
        nc.sync.dma_start(out=query_raw[:], in_=query.rearrange("(p t) q -> p t q", t=PACK))
        pages = sb.tile([P, G // 16], U16, name="pages")
        nc.sync.dma_start(pages[:], offs2)
        nc.sync.dma_start(out=key_rows[:].bitcast(I32)[0:P:8, :], in_=keys_scales[0].bitcast(I32))
        key_pool = sb.tile([P, T], U16, name="key_pool")
        nc.sync.dma_start(out=key_pool[:].bitcast(I32), in_=keys_words[0].bitcast(I32))
        gout_raw = sb.tile([P, PACK, Q], F32, name="gout_raw")
        nc.sync.dma_start(out=gout_raw[:], in_=gout.rearrange("(p t) q -> p t q", t=PACK))

        def pick_key_scales(h):
            key_bytes = sb.tile([P, HALF], U8, name="key_bytes%d" % h)
            nc.vector.tensor_copy(key_bytes[:], key_rows[:].indirect(half_list(h)))
            plane = sb.tile([P, HALF], U8, name="key_plane%d" % h, align_bytes=64)
            nc.vector.memset(plane[:].bitcast(I32), 0)
            for r in range(4):
                nc.sync.dma_start(out=plane[:].bitcast(I32)[r:P:32, :], in_=key_bytes[:].bitcast(I32)[8 * r : P : 32, :])
            return plane

        key_planes = [pick_key_scales(0)]
        ptab_sb = sb.tile([P, U], F32, name="ptab_sb")
        nc.sync.dma_start(out=ptab_sb[:], in_=ptab)
        key_planes.append(pick_key_scales(1))

        val_plane = sb.tile([P, T], U8, name="val_plane")
        nc.vector.memset(val_plane[:].bitcast(I32), 0)
        load_scale_rows(val_plane, vals_scales)
        lam_sb = sb.tile([P, 1], F32, name="lam_sb")
        nc.sync.dma_start(out=lam_sb[:], in_=lam)
        val_pool = sb.tile([P, T], U16, name="val_pool")
        nc.sync.dma_start(out=val_pool[:].bitcast(I32), in_=vals_words[0].bitcast(I32))
        old_sb = sb.tile([P, U], F32, name="old_sb")
        nc.sync.dma_start(out=old_sb[:], in_=old)

        placed = sb.tile([P, U], F32, name="placed")
        nc.vector.memset(placed[:], 0.0)
        lift = sb.tile([P, 2 * G], F32, name="lift")
        nc.vector.memset(lift[:, G:], 0.0)
        ident = sb.tile([P, P], F32, name="ident")
        make_identity(nc, ident[:])

        query_mx = quantise(query_raw, "query", "key_rows_then_query_plane")
        score = []
        for h in range(2):
            key_words = sb.tile([P, HALF], U16, name="key_words%d" % h, align_bytes=64)
            nc.vector.tensor_copy(key_words[:], key_pool[:].indirect(half_list(h)))
            bank = ps.tile([P, HALF], F32, name="score%d" % h)
            mx_product(bank, query_mx, key_words[:], key_planes[h][:])
            score.append(bank)

        pairs = sb.tile([P, PAGE, 2 * G], F32, name="pairs")
        neg_max_first = sb.tile([P, 1], F32, name="neg_max_first")
        neg_max_tile = sb.tile([P, 1], F32, name="neg_max")
        neg_max = neg_max_tile[:]

        def negate_scores(h, start, result):
            nc.vector.tensor_scalar(
                out=pairs[:, :, h * HALF_PAGES : (h + 1) * HALF_PAGES],
                in0=score[h][:].rearrange("p (g j) -> p j g", j=PAGE),
                scalar1=-1.0,
                scalar2=start,
                op0=ALU.mult,
                op1=ALU.min,
                accum_out=result,
            )

        negate_scores(0, None, neg_max_first[:])
        picked = sb.tile([P, G], F32, name="picked")
        nc.vector.tensor_copy(picked[:], ptab_sb[:].indirect(pages[:]))
        negate_scores(1, neg_max_first[:], neg_max)
        gout_mx = quantise(gout_raw, "gout", "gout_plane")

        lam_page = sb.tile([P, 1], F32, name="lam_page")
        nc.scalar.mul(lam_page[:], lam_sb[:], -float(PAGE))
        lam_out = sb.tile([P, 1], F32, name="lam_out")
        nc.scalar.mul(lam_out[:], lam_sb[:], 64.0)
        neg_lam_out = sb.tile([P, 1], F32, name="neg_lam_out")
        nc.scalar.mul(neg_lam_out[:], lam_sb[:], -64.0)

        for first in range(0, PAGE, 4):
            nc.scalar.activation(out=pairs[:, first : first + 4, G:], in_=pairs[:, first : first + 4, :G], func=ACT.Exp, bias=neg_max, scale=-1.0)
        nc.scalar.activation(out=lift[:, :G], in_=picked[:], func=ACT.Copy, scale=lam_page[:])
        weight = []
        for h in range(2):
            r_half = sb.tile([P, HALF], F32, name="weight%d" % h, tag="weight%d" % h)
            nc.scalar.activation(out=r_half[:], in_=score[h][:], func=ACT.Exp, bias=neg_max, scale=1.0)
            weight.append(r_half)

        turned = ps.tile([P, P], F32, name="turned")
        for j in range(PAGE):
            nc.tensor.matmul(turned[:], lhsT=pairs[:, j, :], rhs=ident[:], is_transpose=True, start=(j == 0), stop=False)
        nc.tensor.matmul(turned[:], lhsT=lift[:], rhs=ident[:], is_transpose=True, start=False, stop=True)

        val_bytes = sb.tile([P, I], U8, name="val_bytes", align_bytes=64)
        nc.vector.tensor_copy(val_bytes[:], val_plane[:].indirect(slots[:]))
        val_words = [sb.tile([P, HALF], U16, name="val_words%d" % h, tag="val_words%d" % h, align_bytes=64) for h in range(2)]
        nc.vector.tensor_copy(val_words[0][:], val_pool[:].indirect(half_list(0)))
        back0 = ps.tile([P, HALF], F32, name="back0")
        mx_product(back0, gout_mx, val_words[0][:], val_bytes[:, :HALF])

        nc.vector.tensor_copy(val_words[1][:], val_pool[:].indirect(half_list(1)))
        back1 = ps.tile([P, HALF], F32, name="back1")
        mx_product(back1, gout_mx, val_words[1][:], val_bytes[:, HALF:])
        back = [back0, back1]

        turned_sb = sb.tile([P, P], F32, name="turned_sb", tag="val_words0", align_bytes=64)
        nc.scalar.activation(out=turned_sb[:G, :], in_=turned[:G, :], func=ACT.Sigmoid, scale=-1.0 / PAGE)
        nc.scalar.copy(out=turned_sb[G:, :], in_=turned[G:, :])
        by_row = ps.tile([P, P], F32, name="by_row")
        nc.tensor.transpose(by_row[:], turned_sb[:], ident[:])

        gate = sb.tile([P, G], F32, name="gate")
        nc.scalar.copy(out=gate[:], in_=by_row[:, :G])
        slope = sb.tile([P, G], F32, name="slope")
        nc.scalar.activation(out=slope[:], in_=gate[:], func=ACT.Identity, bias=lam_out[:], scale=neg_lam_out[:])

        page_dot = sb.tile([P, G], F32, name="page_dot")
        prod = [sb.tile([P, HALF], F32, name="prod%d" % h) for h in range(2)]

        def multiply(h):
            nc.vector.tensor_tensor(out=prod[h][:], in0=back[h][:], in1=weight[h][:], op=ALU.mult)

        def sum_pages(h):
            nc.vector.tensor_reduce(
                out=page_dot[:, h * HALF_PAGES : (h + 1) * HALF_PAGES],
                in_=prod[h][:].rearrange("p (g j) -> p g j", j=PAGE),
                axis=AXIS_X,
                op=ALU.add,
            )

        multiply(0)
        sum_pages(0)
        multiply(1)
        mass = sb.tile([P, G], F32, name="mass", tag="weight1")
        total = sb.tile([P, 1], F32, name="total")
        nc.vector.scalar_tensor_tensor(out=mass[:], in0=by_row[:, G:], scalar=1.0, in1=gate[:], op0=ALU.mult, op1=ALU.mult, accum_out=total[:])
        sum_pages(1)
        inv_total = sb.tile([P, 1], F32, name="inv_total")
        nc.vector.reciprocal(inv_total[:], total[:])
        share = sb.tile([P, G], F32, name="share")
        nc.scalar.activation(out=share[:], in_=mass[:], func=ACT.Copy, scale=inv_total[:])
        factor = sb.tile([P, G], F32, name="factor")
        nc.scalar.activation(out=factor[:], in_=slope[:], func=ACT.Copy, scale=inv_total[:])

        neg_gated = sb.tile([P, G], F32, name="neg_gated")
        neg_dot = sb.tile([P, 1], F32, name="neg_dot")
        nc.vector.scalar_tensor_tensor(out=neg_gated[:], in0=page_dot[:], scalar=-1.0, in1=gate[:], op0=ALU.mult, op1=ALU.mult, accum_out=neg_dot[:])
        centred = sb.tile([P, G], F32, name="centred")
        nc.vector.scalar_tensor_tensor(out=centred[:], in0=share[:], scalar=neg_dot[:], in1=neg_gated[:], op0=ALU.mult, op1=ALU.subtract)
        nc.vector.tensor_tensor(placed[:].indirect(pages[:]), centred[:], factor[:], ALU.mult)

        for h, queue in enumerate((nc.sync, nc.scalar)):
            cols = slice(h * U // 2, (h + 1) * U // 2)
            result = sb.tile([P, U // 2], F32, name="result%d" % h)
            nc.vector.tensor_tensor(out=result[:], in0=placed[:, cols], in1=old_sb[:, cols], op=ALU.add)
            queue.dma_start(out=out[:, cols], in_=result[:])
